import numpy as np
import ml_dtypes


def mxq(x, axis, fmt="e4m3"):
    dtype, down = {"e4m3": (ml_dtypes.float8_e4m3fn, 7), "e5m2": (ml_dtypes.float8_e5m2, 14)}[fmt]
    v = np.moveaxis(np.asarray(x, np.float32).astype(ml_dtypes.bfloat16).astype(np.float64), axis, -1)
    blocks = v.reshape(v.shape[:-1] + (-1, 32))
    amax = np.abs(blocks).max(-1, keepdims=True)
    byte = np.maximum(np.where(amax > 0, np.frexp(amax)[1] - 1 + 127, 0) - down, 1)
    scale = np.exp2(byte - 127.0)
    codes = (blocks / scale).astype(np.float32).astype(dtype).astype(np.float64)
    return np.moveaxis((codes * scale).reshape(v.shape), -1, axis)


WIDE = False


def mx_kscale(k):
    if not WIDE:
        return np.ones(k)
    levels = np.array([10, -10, 5, -5, 0])
    if k % 512:
        return np.exp2(np.random.permutation(np.resize(levels, k // 32))).repeat(32)
    a = np.empty((k // 512, 16))
    for p in range(k // 512):
        a[p, :8] = np.random.permutation(np.resize(levels, 8))
        for g in range(8):
            far = levels[np.abs(levels - a[p, g]) >= 10]
            a[p, g + 8] = far[np.random.randint(len(far))]
    return np.exp2(a.ravel()).repeat(32)


def f64(x):
    return np.asarray(x).astype(np.float64)


def striped(idx):
    return np.tile(np.asarray(idx).reshape(-1, 16).T, (8, 1)).astype(np.uint16)


def unstriped(offs):
    return offs[:16].T.reshape(-1).astype(np.int64)


E2M1 = np.array([0.0, 0.5, 1.0, 1.5, 2.0, 3.0, 4.0, 6.0, -0.0, -0.5, -1.0, -1.5, -2.0, -3.0, -4.0, -6.0])


def pack_weight(w, fmt):
    k, n = w.shape
    w = f64(np.asarray(w, np.float32).astype(ml_dtypes.bfloat16)).reshape(k // 32, 32, n)
    amax = np.abs(w).max(1)
    if fmt == "e4m3":
        byte = np.frexp(amax)[1] - 1 + 127 - 7
    else:
        mant, ex = np.frexp(amax / 6.0)
        byte = np.where(mant > 0.5, ex, ex - 1) + 127
    byte = np.clip(np.where(amax > 0, byte, 1), 1, 254)
    scaled = (w * np.exp2(127.0 - byte)[:, None, :]).reshape(k, n).astype(np.float32)
    by_word = np.ascontiguousarray(scaled.reshape(k // 512, 128, 4, n).transpose(0, 1, 3, 2))
    if fmt == "e4m3":
        words = by_word.astype(ml_dtypes.float8_e4m3fn).view(np.uint8)
    else:
        c = by_word.astype(ml_dtypes.float4_e2m1fn).view(np.uint8) & 0xF
        words = (c[..., 0::2] | (c[..., 1::2] << 4)).reshape(k // 512, 128, 2 * n)
    return np.ascontiguousarray(words), np.ascontiguousarray(byte.astype(np.uint8).reshape(k // 512, 16, n))


def unpack_weight(words, scales, fmt):
    g, _, n = scales.shape
    words = np.ascontiguousarray(words).reshape(g, 128, n, -1)
    if fmt == "e4m3":
        vals = words.view(ml_dtypes.float8_e4m3fn).astype(np.float64)
    else:
        nib = np.empty((g, 128, n, 4), np.uint8)
        nib[..., 0::2] = words & 0xF
        nib[..., 1::2] = words >> 4
        vals = E2M1[nib]
    vals = vals * np.repeat(np.exp2(scales.astype(np.float64) - 127.0), 8, axis=1)[..., None]
    return vals.transpose(0, 1, 3, 2).reshape(g * 512, n)


def sigmoid(v):
    return 1.0 / (1.0 + np.exp(-v))


K, L, T, C, J = 512, 512, 512, 1024, 512


def setup_inputs():
    n = np.random.standard_normal
    idx = np.random.permutation(C)[:J]
    idx2 = np.random.permutation(C)[:J]
    fk = mx_kscale(K)
    fl = mx_kscale(L)
    wcp = pack_weight(n((K, C)) * 1 / np.sqrt(K) * fk[:, None], "e2m1")
    xsp = pack_weight(n((L, T)) / fl[:, None], "e4m3")
    wsp = pack_weight(n((L, J)) * 1 / np.sqrt(L) * fl[:, None], "e2m1")
    return {
        "xt": (n((K, T)) / fk[:, None]).astype(np.float32),
        "wc_words": wcp[0],
        "wc_scales": wcp[1],
        "xs_words": xsp[0],
        "xs_scales": xsp[1],
        "ws_words": wsp[0],
        "ws_scales": wsp[1],
        "offs": striped(idx),
        "offs2": striped(idx2),
    }


def reference(xt, wc_words, wc_scales, xs_words, xs_scales, ws_words, ws_scales, offs, offs2):
    idx = unstriped(offs)
    idx2 = unstriped(offs2)
    wcu = unpack_weight(wc_words, wc_scales, "e2m1")
    xsu = unpack_weight(xs_words, xs_scales, "e4m3")
    wsu = unpack_weight(ws_words, ws_scales, "e2m1")
    xtq = mxq(f64(xt), 0, "e4m3")
    z = xtq.T @ wcu
    s = xsu.T @ wsu
    y = z[:, idx] * sigmoid(z[:, idx2]) * s
    return y

@@ -1,0 +1,168 @@
+from contextlib import ExitStack
+
+import concourse.mybir as mybir
+
+K, L, T, C, J = 512, 512, 512, 1024, 512
+FLOPS = 2 * T * (K * C + L * J)
+
+F32 = mybir.dt.float32
+BF16 = mybir.dt.bfloat16
+I32 = mybir.dt.int32
+U32 = mybir.dt.uint32
+U16 = mybir.dt.uint16
+U8 = mybir.dt.uint8
+FP8X4 = mybir.dt.float8_e4m3fn_x4
+FP4X4 = mybir.dt.float4_e2m1fn_x4
+MULT = mybir.AluOpType.mult
+SIGMOID = mybir.ActivationFunctionType.Sigmoid
+
+P = 128
+PACK = 4
+BANK = 512
+TILES = T // P
+HALF = J // 2
+HCOLS = HALF // 16
+
+
+def load_scales(queue, plane, scales):
+    for q in range(4):
+        queue.dma_start(out=plane[32 * q : 32 * q + 4, :].bitcast(I32), in_=scales[0, 4 * q : 4 * q + 4, :].bitcast(I32))
+
+
+def tile_list_two_pickers_one_row_kernel(tc, xt, wc_words, wc_scales, xs_words, xs_scales, ws_words, ws_scales, offs, offs2, out):
+    nc = tc.nc
+    with ExitStack() as ctx:
+        keep = ctx.enter_context(tc.tile_pool(name="keep", bufs=1))
+        ring = ctx.enter_context(tc.tile_pool(name="ring", bufs=2))
+        zps = ctx.enter_context(tc.psum_pool(name="zps", bufs=6))
+        sps = ctx.enter_context(tc.psum_pool(name="sps", bufs=2))
+
+        wc_plane = keep.tile([P, C], U8, align_bytes=64)
+        xs_plane = keep.tile([P, T], U8, align_bytes=64)
+        ws_plane = keep.tile([P, J], U8, align_bytes=64)
+        nc.vector.memset(wc_plane[:].bitcast(I32), 0)
+        nc.vector.memset(ws_plane[:].bitcast(I32), 0)
+        nc.gpsimd.memset(xs_plane[:].bitcast(I32), 0)
+        warm = keep.tile([P, 8], F32)
+        nc.vector.memset(warm[:], 0.0)
+        warmed = keep.tile([P, 8], F32)
+        nc.scalar.activation(warmed[:], warm[:], SIGMOID)
+
+        x_rows = xt.rearrange("(p j) t -> p j t", j=PACK)
+        spans = [(0, 1), (1, 2), (2, 4)]
+        raw = [keep.tile([P, PACK, P * (b - a)], F32, name="raw%d" % a) for a, b in spans]
+        wc = keep.tile([P, 2 * C], U8, align_bytes=64)
+        xs = keep.tile([P, PACK * T], U8, align_bytes=64)
+        ws = keep.tile([P, 2 * J], U8, align_bytes=64)
+        pick = keep.tile([P, J // 16], U16)
+        gate_pick = keep.tile([P, J // 16], U16)
+
+        def load_x(n):
+            a, b = spans[n]
+            nc.sync.dma_start(out=raw[n][:], in_=x_rows[:, :, P * a : P * b])
+
+        load_x(0)
+        load_scales(nc.gpsimd, xs_plane, xs_scales)
+        nc.sync.dma_start(out=wc[:].bitcast(I32), in_=wc_words[0].bitcast(I32))
+        load_scales(nc.sync, wc_plane, wc_scales)
+        load_x(1)
+        load_x(2)
+        nc.sync.dma_start(gate_pick[:], offs2)
+        nc.sync.dma_start(pick[:], offs)
+        nc.sync.dma_start(out=ws[:].bitcast(I32), in_=ws_words[0].bitcast(I32))
+        nc.sync.dma_start(out=xs[:].bitcast(I32), in_=xs_words[0].rearrange("p t r -> p (t r)").bitcast(I32))
+        load_scales(nc.sync, ws_plane, ws_scales)
+
+
+        codes, planes, z_banks, s_banks, z, gate, gated, res = {}, {}, {}, {}, {}, {}, {}, {}
+
+        def quantise(n):
+            a, b = spans[n]
+            width = P * (b - a)
+            grouped = keep.tile([P, width, PACK], BF16, name="grouped%d" % n, align_bytes=64)
+            nc.vector.tensor_copy(out=grouped[:], in_=raw[n][:].rearrange("p j t -> p t j"))
+            words = keep.tile([P, width], U32, name="codes%d" % n, align_bytes=64)
+            plane = keep.tile([P, width], U8, name="plane%d" % n, align_bytes=64)
+            nc.vector.quantize_mx(out=words[:].bitcast(FP8X4), scales=plane[:], in_=grouped[:].rearrange("p t j -> p (t j)"))
+            for i in range(a, b):
+                codes[i] = words[:, P * (i - a) : P * (i - a + 1)]
+                planes[i] = plane[:, P * (i - a) : P * (i - a + 1)]
+
+        def z_product(i):
+            z_banks[i] = []
+            for h in range(C // BANK):
+                bank = zps.tile([P, BANK], F32, name="zbank")
+                nc.tensor.matmul_mx(
+                    out=bank[:],
+                    lhsT=codes[i].bitcast(FP8X4),
+                    lhsT_scale=planes[i],
+                    rhs=wc[:, 2 * BANK * h : 2 * BANK * (h + 1)].bitcast(FP4X4),
+                    rhs_scale=wc_plane[:, BANK * h : BANK * (h + 1)],
+                    start=True,
+                    stop=True,
+                )
+                z_banks[i].append(bank)
+
+        def s_product(i):
+            s_banks[i] = sps.tile([P, J], F32, name="sbank")
+            nc.tensor.matmul_mx(
+                out=s_banks[i][:],
+                lhsT=xs[:, PACK * P * i : PACK * P * (i + 1)].bitcast(FP8X4),
+                lhsT_scale=xs_plane[:, P * i : P * (i + 1)],
+                rhs=ws[:].bitcast(FP4X4),
+                rhs_scale=ws_plane[:],
+                start=True,
+                stop=True,
+            )
+
+        def z_out(i, h, on_vector):
+            if i not in z:
+                z[i] = keep.tile([P, C], F32, name="z%d" % i)
+            if on_vector:
+                nc.vector.tensor_copy(out=z[i][:, BANK * h : BANK * (h + 1)], in_=z_banks[i][h][:])
+            else:
+                nc.scalar.copy(out=z[i][:, BANK * h : BANK * (h + 1)], in_=z_banks[i][h][:])
+
+        def gate_of(i):
+            for u in range(2):
+                gate[i, u] = keep.tile([P, HALF], F32, name="gate%d_%d" % (i, u))
+                nc.scalar.activation(gate[i, u][:], z[i][:].indirect(gate_pick[:, HCOLS * u : HCOLS * (u + 1)]), SIGMOID)
+
+        def finish(i):
+            res[i] = keep.tile([P, J], F32, name="res%d" % i)
+            for u in range(2):
+                gated[i, u] = ring.tile([P, HALF], F32, name="gated")
+                nc.vector.tensor_tensor(gated[i, u][:], z[i][:].indirect(pick[:, HCOLS * u : HCOLS * (u + 1)]), gate[i, u][:], MULT)
+            for u in range(2):
+                cols = slice(HALF * u, HALF * (u + 1))
+                nc.vector.tensor_tensor(res[i][:, cols], gated[i, u][:], s_banks[i][:, cols], MULT)
+                if i == TILES - 1:
+                    nc.sync.dma_start(out=out[P * i : P * (i + 1), cols], in_=res[i][:, cols])
+            if i < TILES - 1:
+                nc.sync.dma_start(out=out[P * i : P * (i + 1), :], in_=res[i][:])
+
+        quantise(0)
+        z_product(0)
+        quantise(1)
+        z_product(1)
+        z_out(0, 0, False)
+        z_out(0, 1, False)
+        gate_of(0)
+        quantise(2)
+        z_out(1, 0, True)
+        z_out(1, 1, True)
+        z_product(2)
+        z_product(3)
+        for i in range(TILES):
+            s_product(i)
+        gate_of(1)
+        finish(0)
+        z_out(2, 0, False)
+        z_out(2, 1, False)
+        gate_of(2)
+        finish(1)
+        z_out(3, 0, False)
+        z_out(3, 1, False)
+        gate_of(3)
+        finish(2)
+        finish(3)

@@ -33,9 +33,9 @@ def tile_list_two_pickers_one_row_kernel(tc, xt, wc_words, wc_scales, xs_words, 
     nc = tc.nc
     with ExitStack() as ctx:
         keep = ctx.enter_context(tc.tile_pool(name="keep", bufs=1))
-        ring = ctx.enter_context(tc.tile_pool(name="ring", bufs=2))
-        zps = ctx.enter_context(tc.psum_pool(name="zps", bufs=6))
-        sps = ctx.enter_context(tc.psum_pool(name="sps", bufs=2))
+        ring = ctx.enter_context(tc.tile_pool(name="ring", bufs=4))
+        zps = ctx.enter_context(tc.psum_pool(name="zps", bufs=5))
+        sps = ctx.enter_context(tc.psum_pool(name="sps", bufs=3))
 
         wc_plane = keep.tile([P, C], U8, align_bytes=64)
         xs_plane = keep.tile([P, T], U8, align_bytes=64)
@@ -68,11 +68,10 @@ def tile_list_two_pickers_one_row_kernel(tc, xt, wc_words, wc_scales, xs_words, 
         load_x(1)
         load_x(2)
         nc.sync.dma_start(gate_pick[:], offs2)
-        nc.sync.dma_start(pick[:], offs)
-        nc.sync.dma_start(out=ws[:].bitcast(I32), in_=ws_words[0].bitcast(I32))
         nc.sync.dma_start(out=xs[:].bitcast(I32), in_=xs_words[0].rearrange("p t r -> p (t r)").bitcast(I32))
+        nc.sync.dma_start(out=ws[:].bitcast(I32), in_=ws_words[0].bitcast(I32))
+        nc.sync.dma_start(pick[:], offs)
         load_scales(nc.sync, ws_plane, ws_scales)
-
 
         codes, planes, z_banks, s_banks, z, gate, gated, res = {}, {}, {}, {}, {}, {}, {}, {}
 
@@ -123,21 +122,33 @@ def tile_list_two_pickers_one_row_kernel(tc, xt, wc_words, wc_scales, xs_words, 
             else:
                 nc.scalar.copy(out=z[i][:, BANK * h : BANK * (h + 1)], in_=z_banks[i][h][:])
 
+        def pieces(i):
+            cuts = [0, 256, 384, 512] if i == TILES - 1 else [0, 256, 512]
+            return list(zip(cuts[:-1], cuts[1:]))
+
         def gate_of(i):
-            for u in range(2):
-                gate[i, u] = keep.tile([P, HALF], F32, name="gate%d_%d" % (i, u))
-                nc.scalar.activation(gate[i, u][:], z[i][:].indirect(gate_pick[:, HCOLS * u : HCOLS * (u + 1)]), SIGMOID)
+            for a, b in pieces(i):
+                gate[i, a] = keep.tile([P, b - a], F32, name="gate%d_%d" % (i, a))
+                nc.scalar.activation(gate[i, a][:], z[i][:].indirect(gate_pick[:, a // 16 : b // 16]), SIGMOID)
 
         def finish(i):
             res[i] = keep.tile([P, J], F32, name="res%d" % i)
-            for u in range(2):
-                gated[i, u] = ring.tile([P, HALF], F32, name="gated")
-                nc.vector.tensor_tensor(gated[i, u][:], z[i][:].indirect(pick[:, HCOLS * u : HCOLS * (u + 1)]), gate[i, u][:], MULT)
-            for u in range(2):
-                cols = slice(HALF * u, HALF * (u + 1))
-                nc.vector.tensor_tensor(res[i][:, cols], gated[i, u][:], s_banks[i][:, cols], MULT)
+
+            def gather(a, b):
+                gated[i, a] = ring.tile([P, b - a], F32, name="gated")
+                nc.vector.tensor_tensor(gated[i, a][:], z[i][:].indirect(pick[:, a // 16 : b // 16]), gate[i, a][:], MULT)
+
+            def scale(a, b):
+                nc.vector.tensor_tensor(res[i][:, a:b], gated[i, a][:], s_banks[i][:, a:b], MULT)
                 if i == TILES - 1:
-                    nc.sync.dma_start(out=out[P * i : P * (i + 1), cols], in_=res[i][:, cols])
+                    nc.sync.dma_start(out=out[P * i : P * (i + 1), a:b], in_=res[i][:, a:b])
+
+            cut = pieces(i)
+            gather(*cut[0])
+            for n in range(1, len(cut)):
+                gather(*cut[n])
+                scale(*cut[n - 1])
+            scale(*cut[-1])
             if i < TILES - 1:
                 nc.sync.dma_start(out=out[P * i : P * (i + 1), :], in_=res[i][:])
 
@@ -155,13 +166,13 @@ def tile_list_two_pickers_one_row_kernel(tc, xt, wc_words, wc_scales, xs_words, 
         z_product(3)
         for i in range(TILES):
             s_product(i)
+        z_out(2, 0, False)
         gate_of(1)
         finish(0)
-        z_out(2, 0, False)
         z_out(2, 1, False)
+        z_out(3, 0, False)
         gate_of(2)
         finish(1)
-        z_out(3, 0, False)
         z_out(3, 1, False)
         gate_of(3)
         finish(2)

@@ -14,6 +14,7 @@ U8 = mybir.dt.uint8
 FP8X4 = mybir.dt.float8_e4m3fn_x4
 FP4X4 = mybir.dt.float4_e2m1fn_x4
 MULT = mybir.AluOpType.mult
+ADD = mybir.AluOpType.add
 SIGMOID = mybir.ActivationFunctionType.Sigmoid
 
 P = 128
@@ -49,7 +50,7 @@ def tile_list_two_pickers_one_row_kernel(tc, xt, wc_words, wc_scales, xs_words, 
         nc.scalar.activation(warmed[:], warm[:], SIGMOID)
 
         x_rows = xt.rearrange("(p j) t -> p j t", j=PACK)
-        spans = [(0, 1), (1, 2), (2, 4)]
+        spans = [(0, 1), (1, 2), (2, 3), (3, 4)]
         raw = [keep.tile([P, PACK, P * (b - a)], F32, name="raw%d" % a) for a, b in spans]
         wc = keep.tile([P, 2 * C], U8, align_bytes=64)
         xs = keep.tile([P, PACK * T], U8, align_bytes=64)
@@ -62,16 +63,17 @@ def tile_list_two_pickers_one_row_kernel(tc, xt, wc_words, wc_scales, xs_words, 
             nc.sync.dma_start(out=raw[n][:], in_=x_rows[:, :, P * a : P * b])
 
         load_x(0)
-        load_scales(nc.gpsimd, xs_plane, xs_scales)
         nc.sync.dma_start(out=wc[:].bitcast(I32), in_=wc_words[0].bitcast(I32))
         load_scales(nc.sync, wc_plane, wc_scales)
         load_x(1)
         load_x(2)
         nc.sync.dma_start(gate_pick[:], offs2)
+        load_x(3)
         nc.sync.dma_start(out=xs[:].bitcast(I32), in_=xs_words[0].rearrange("p t r -> p (t r)").bitcast(I32))
         nc.sync.dma_start(out=ws[:].bitcast(I32), in_=ws_words[0].bitcast(I32))
-        nc.sync.dma_start(pick[:], offs)
         load_scales(nc.sync, ws_plane, ws_scales)
+        nc.sync.dma_start(pick[:], offs)
+        load_scales(nc.sync, xs_plane, xs_scales)
 
         codes, planes, z_banks, s_banks, z, gate, gated, res = {}, {}, {}, {}, {}, {}, {}, {}
 
@@ -79,7 +81,10 @@ def tile_list_two_pickers_one_row_kernel(tc, xt, wc_words, wc_scales, xs_words, 
             a, b = spans[n]
             width = P * (b - a)
             grouped = keep.tile([P, width, PACK], BF16, name="grouped%d" % n, align_bytes=64)
-            nc.vector.tensor_copy(out=grouped[:], in_=raw[n][:].rearrange("p j t -> p t j"))
+            if n == 3:
+                nc.gpsimd.tensor_scalar(grouped[:], raw[n][:].rearrange("p j t -> p t j"), 1.0, 0.0, MULT, ADD)
+            else:
+                nc.vector.tensor_copy(out=grouped[:], in_=raw[n][:].rearrange("p j t -> p t j"))
             words = keep.tile([P, width], U32, name="codes%d" % n, align_bytes=64)
             plane = keep.tile([P, width], U8, name="plane%d" % n, align_bytes=64)
             nc.vector.quantize_mx(out=words[:].bitcast(FP8X4), scales=plane[:], in_=grouped[:].rearrange("p t j -> p (t j)"))
@@ -158,11 +163,12 @@ def tile_list_two_pickers_one_row_kernel(tc, xt, wc_words, wc_scales, xs_words, 
         z_product(1)
         z_out(0, 0, False)
         z_out(0, 1, False)
-        gate_of(0)
         quantise(2)
+        gate_of(0)
         z_out(1, 0, True)
         z_out(1, 1, True)
         z_product(2)
+        quantise(3)
         z_product(3)
         for i in range(TILES):
             s_product(i)

@@ -69,11 +69,11 @@ def tile_list_two_pickers_one_row_kernel(tc, xt, wc_words, wc_scales, xs_words, 
         load_x(2)
         nc.sync.dma_start(gate_pick[:], offs2)
         load_x(3)
+        load_scales(nc.sync, xs_plane, xs_scales)
+        nc.sync.dma_start(pick[:], offs)
         nc.sync.dma_start(out=xs[:].bitcast(I32), in_=xs_words[0].rearrange("p t r -> p (t r)").bitcast(I32))
         nc.sync.dma_start(out=ws[:].bitcast(I32), in_=ws_words[0].bitcast(I32))
         load_scales(nc.sync, ws_plane, ws_scales)
-        nc.sync.dma_start(pick[:], offs)
-        load_scales(nc.sync, xs_plane, xs_scales)
 
         codes, planes, z_banks, s_banks, z, gate, gated, res = {}, {}, {}, {}, {}, {}, {}, {}
 
@@ -128,7 +128,7 @@ def tile_list_two_pickers_one_row_kernel(tc, xt, wc_words, wc_scales, xs_words, 
                 nc.scalar.copy(out=z[i][:, BANK * h : BANK * (h + 1)], in_=z_banks[i][h][:])
 
         def pieces(i):
-            cuts = [0, 256, 384, 512] if i == TILES - 1 else [0, 256, 512]
+            cuts = [0, 128, 256, 384, 512] if i == TILES - 1 else [0, 256, 512]
             return list(zip(cuts[:-1], cuts[1:]))
 
         def gate_of(i):
@@ -166,7 +166,7 @@ def tile_list_two_pickers_one_row_kernel(tc, xt, wc_words, wc_scales, xs_words, 
         quantise(2)
         gate_of(0)
         z_out(1, 0, True)
-        z_out(1, 1, True)
+        z_out(1, 1, False)
         z_product(2)
         quantise(3)
         z_product(3)

from contextlib import ExitStack

import concourse.mybir as mybir

K, L, T, C, J = 512, 512, 512, 1024, 512
FLOPS = 2 * T * (K * C + L * J)

F32 = mybir.dt.float32
BF16 = mybir.dt.bfloat16
I32 = mybir.dt.int32
U32 = mybir.dt.uint32
U16 = mybir.dt.uint16
U8 = mybir.dt.uint8
FP8X4 = mybir.dt.float8_e4m3fn_x4
FP4X4 = mybir.dt.float4_e2m1fn_x4
MULT = mybir.AluOpType.mult
ADD = mybir.AluOpType.add
SIGMOID = mybir.ActivationFunctionType.Sigmoid

P = 128
PACK = 4
BANK = 512
TILES = T // P
HALF = J // 2
HCOLS = HALF // 16


def load_scales(queue, plane, scales):
    for q in range(4):
        queue.dma_start(out=plane[32 * q : 32 * q + 4, :].bitcast(I32), in_=scales[0, 4 * q : 4 * q + 4, :].bitcast(I32))


def tile_list_two_pickers_one_row_kernel(tc, xt, wc_words, wc_scales, xs_words, xs_scales, ws_words, ws_scales, offs, offs2, out):
    nc = tc.nc
    with ExitStack() as ctx:
        keep = ctx.enter_context(tc.tile_pool(name="keep", bufs=1))
        ring = ctx.enter_context(tc.tile_pool(name="ring", bufs=4))
        zps = ctx.enter_context(tc.psum_pool(name="zps", bufs=5))
        sps = ctx.enter_context(tc.psum_pool(name="sps", bufs=3))

        wc_plane = keep.tile([P, C], U8, align_bytes=64)
        xs_plane = keep.tile([P, T], U8, align_bytes=64)
        ws_plane = keep.tile([P, J], U8, align_bytes=64)
        nc.vector.memset(wc_plane[:].bitcast(I32), 0)
        nc.vector.memset(ws_plane[:].bitcast(I32), 0)
        nc.gpsimd.memset(xs_plane[:].bitcast(I32), 0)
        warm = keep.tile([P, 8], F32)
        nc.vector.memset(warm[:], 0.0)
        warmed = keep.tile([P, 8], F32)
        nc.scalar.activation(warmed[:], warm[:], SIGMOID)

        x_rows = xt.rearrange("(p j) t -> p j t", j=PACK)
        spans = [(0, 1), (1, 2), (2, 3), (3, 4)]
        raw = [keep.tile([P, PACK, P * (b - a)], F32, name="raw%d" % a) for a, b in spans]
        wc = keep.tile([P, 2 * C], U8, align_bytes=64)
        xs = keep.tile([P, PACK * T], U8, align_bytes=64)
        ws = keep.tile([P, 2 * J], U8, align_bytes=64)
        pick = keep.tile([P, J // 16], U16)
        gate_pick = keep.tile([P, J // 16], U16)

        def load_x(n):
            a, b = spans[n]
            nc.sync.dma_start(out=raw[n][:], in_=x_rows[:, :, P * a : P * b])

        load_x(0)
        nc.sync.dma_start(out=wc[:].bitcast(I32), in_=wc_words[0].bitcast(I32))
        load_scales(nc.sync, wc_plane, wc_scales)
        load_x(1)
        load_x(2)
        nc.sync.dma_start(gate_pick[:], offs2)
        load_x(3)
        load_scales(nc.sync, xs_plane, xs_scales)
        nc.sync.dma_start(pick[:], offs)
        nc.sync.dma_start(out=xs[:].bitcast(I32), in_=xs_words[0].rearrange("p t r -> p (t r)").bitcast(I32))
        nc.sync.dma_start(out=ws[:].bitcast(I32), in_=ws_words[0].bitcast(I32))
        load_scales(nc.sync, ws_plane, ws_scales)

        codes, planes, z_banks, s_banks, z, gate, gated, res = {}, {}, {}, {}, {}, {}, {}, {}

        def quantise(n):
            a, b = spans[n]
            width = P * (b - a)
            grouped = keep.tile([P, width, PACK], BF16, name="grouped%d" % n, align_bytes=64)
            if n == 3:
                nc.gpsimd.tensor_scalar(grouped[:], raw[n][:].rearrange("p j t -> p t j"), 1.0, 0.0, MULT, ADD)
            else:
                nc.vector.tensor_copy(out=grouped[:], in_=raw[n][:].rearrange("p j t -> p t j"))
            words = keep.tile([P, width], U32, name="codes%d" % n, align_bytes=64)
            plane = keep.tile([P, width], U8, name="plane%d" % n, align_bytes=64)
            nc.vector.quantize_mx(out=words[:].bitcast(FP8X4), scales=plane[:], in_=grouped[:].rearrange("p t j -> p (t j)"))
            for i in range(a, b):
                codes[i] = words[:, P * (i - a) : P * (i - a + 1)]
                planes[i] = plane[:, P * (i - a) : P * (i - a + 1)]

        def z_product(i):
            z_banks[i] = []
            for h in range(C // BANK):
                bank = zps.tile([P, BANK], F32, name="zbank")
                nc.tensor.matmul_mx(
                    out=bank[:],
                    lhsT=codes[i].bitcast(FP8X4),
                    lhsT_scale=planes[i],
                    rhs=wc[:, 2 * BANK * h : 2 * BANK * (h + 1)].bitcast(FP4X4),
                    rhs_scale=wc_plane[:, BANK * h : BANK * (h + 1)],
                    start=True,
                    stop=True,
                )
                z_banks[i].append(bank)

        def s_product(i):
            s_banks[i] = sps.tile([P, J], F32, name="sbank")
            nc.tensor.matmul_mx(
                out=s_banks[i][:],
                lhsT=xs[:, PACK * P * i : PACK * P * (i + 1)].bitcast(FP8X4),
                lhsT_scale=xs_plane[:, P * i : P * (i + 1)],
                rhs=ws[:].bitcast(FP4X4),
                rhs_scale=ws_plane[:],
                start=True,
                stop=True,
            )

        def z_out(i, h, on_vector):
            if i not in z:
                z[i] = keep.tile([P, C], F32, name="z%d" % i)
            if on_vector:
                nc.vector.tensor_copy(out=z[i][:, BANK * h : BANK * (h + 1)], in_=z_banks[i][h][:])
            else:
                nc.scalar.copy(out=z[i][:, BANK * h : BANK * (h + 1)], in_=z_banks[i][h][:])

        def pieces(i):
            cuts = [0, 128, 256, 384, 512] if i == TILES - 1 else [0, 256, 512]
            return list(zip(cuts[:-1], cuts[1:]))

        def gate_of(i):
            for a, b in pieces(i):
                gate[i, a] = keep.tile([P, b - a], F32, name="gate%d_%d" % (i, a))
                nc.scalar.activation(gate[i, a][:], z[i][:].indirect(gate_pick[:, a // 16 : b // 16]), SIGMOID)

        def finish(i):
            res[i] = keep.tile([P, J], F32, name="res%d" % i)

            def gather(a, b):
                gated[i, a] = ring.tile([P, b - a], F32, name="gated")
                nc.vector.tensor_tensor(gated[i, a][:], z[i][:].indirect(pick[:, a // 16 : b // 16]), gate[i, a][:], MULT)

            def scale(a, b):
                nc.vector.tensor_tensor(res[i][:, a:b], gated[i, a][:], s_banks[i][:, a:b], MULT)
                if i == TILES - 1:
                    nc.sync.dma_start(out=out[P * i : P * (i + 1), a:b], in_=res[i][:, a:b])

            cut = pieces(i)
            gather(*cut[0])
            for n in range(1, len(cut)):
                gather(*cut[n])
                scale(*cut[n - 1])
            scale(*cut[-1])
            if i < TILES - 1:
                nc.sync.dma_start(out=out[P * i : P * (i + 1), :], in_=res[i][:])

        quantise(0)
        z_product(0)
        quantise(1)
        z_product(1)
        z_out(0, 0, False)
        z_out(0, 1, False)
        quantise(2)
        gate_of(0)
        z_out(1, 0, True)
        z_out(1, 1, False)
        z_product(2)
        quantise(3)
        z_product(3)
        for i in range(TILES):
            s_product(i)
        z_out(2, 0, False)
        gate_of(1)
        finish(0)
        z_out(2, 1, False)
        z_out(3, 0, False)
        gate_of(2)
        finish(1)
        z_out(3, 1, False)
        gate_of(3)
        finish(2)
        finish(3)
